import numpy as np
import ml_dtypes


def mxq(x, axis, fmt="e4m3"):
    dtype, down = {"e4m3": (ml_dtypes.float8_e4m3fn, 7), "e5m2": (ml_dtypes.float8_e5m2, 14)}[fmt]
    v = np.moveaxis(np.asarray(x, np.float32).astype(ml_dtypes.bfloat16).astype(np.float64), axis, -1)
    blocks = v.reshape(v.shape[:-1] + (-1, 32))
    amax = np.abs(blocks).max(-1, keepdims=True)
    byte = np.maximum(np.where(amax > 0, np.frexp(amax)[1] - 1 + 127, 0) - down, 1)
    scale = np.exp2(byte - 127.0)
    codes = (blocks / scale).astype(np.float32).astype(dtype).astype(np.float64)
    return np.moveaxis((codes * scale).reshape(v.shape), -1, axis)


WIDE = False


def mx_kscale(k):
    if not WIDE:
        return np.ones(k)
    levels = np.array([10, -10, 5, -5, 0])
    if k % 512:
        return np.exp2(np.random.permutation(np.resize(levels, k // 32))).repeat(32)
    a = np.empty((k // 512, 16))
    for p in range(k // 512):
        a[p, :8] = np.random.permutation(np.resize(levels, 8))
        for g in range(8):
            far = levels[np.abs(levels - a[p, g]) >= 10]
            a[p, g + 8] = far[np.random.randint(len(far))]
    return np.exp2(a.ravel()).repeat(32)


BF16 = ml_dtypes.bfloat16


def bf(x):
    return np.asarray(x, np.float32).astype(BF16)


def f64(x):
    return np.asarray(x).astype(np.float64)

E4M3FN = np.array([(-1.0 if i & 128 else 1.0) * ((1.0 + (i & 7) / 8.0) * 2.0 ** (((i >> 3) & 15) - 7) if i & 120 else (i & 7) * 2.0 ** -9) for i in range(256)])


def e4m3fn_bytes(y):
    return np.clip(np.asarray(y, np.float64), -448.0, 448.0).astype(np.float32).astype(ml_dtypes.float8_e4m3fn).view(np.uint8)


def e4m3fn_values(b):
    return E4M3FN[b]


V, F, O, B = 1536, 1024, 512, 128


def setup_inputs():
    s, t = mx_kscale(V), mx_kscale(F)
    G = np.random.standard_normal((V, V))
    L = (G + G.T) / np.sqrt(8 * V) * s
    theta = np.random.standard_normal((F, O)) / np.sqrt(F) / t[:, None]
    L_scale = (np.abs(L).reshape(V // B, B, V // B, B).max(axis=(1, 3)) / 448).astype(np.float32)
    theta_scale = (np.abs(theta).reshape(F // B, B, O // B, B).max(axis=(1, 3)) / 448).astype(np.float32)
    L_bytes = e4m3fn_bytes(L / np.repeat(np.repeat(f64(L_scale), B, axis=0), B, axis=1))
    theta_bytes = e4m3fn_bytes(theta / np.repeat(np.repeat(f64(theta_scale), B, axis=0), B, axis=1))
    return {"L_bytes": L_bytes,
            "L_scale": L_scale,
            "t1": bf(np.random.standard_normal((V, F)) / s[:, None] * t),
            "t0": bf(np.random.standard_normal((V, F)) * t),
            "theta_bytes": theta_bytes,
            "theta_scale": theta_scale,
            "acc": bf(np.random.standard_normal((V, O)))}


def reference(L_bytes, L_scale, t1, t0, theta_bytes, theta_scale, acc):
    L = e4m3fn_values(L_bytes) * np.repeat(np.repeat(f64(L_scale), B, axis=0), B, axis=1)
    theta = e4m3fn_values(theta_bytes) * np.repeat(np.repeat(f64(theta_scale), B, axis=0), B, axis=1)
    p = mxq(L, 1, "e4m3") @ mxq(f64(t1), 0, "e4m3")
    z = 2.0 * p - f64(t0)
    y = mxq(z, 1, "e4m3") @ mxq(theta, 0, "e4m3")
    return np.maximum(f64(acc) + y, 0.0)

@@ -1,0 +1,370 @@
+from contextlib import ExitStack
+
+import concourse.mybir as mybir
+from concourse.masks import make_identity
+
+V, F, O = 1536, 1024, 512
+FLOPS = 2 * V * V * F + 2 * V * F * O
+
+F32 = mybir.dt.float32
+BF16 = mybir.dt.bfloat16
+U32 = mybir.dt.uint32
+U8 = mybir.dt.uint8
+FP8 = mybir.dt.float8_e4m3fn
+FP8X4 = mybir.dt.float8_e4m3fn_x4
+ACT = mybir.ActivationFunctionType
+ALU = mybir.AluOpType
+
+P = 128
+NT = V // P
+NP = NT // 2
+G1 = V // 512
+G2 = F // 512
+HEAD = 4
+WV = (0, 3, 4, 5, 7, 9, 10)
+T1A = ((1, 1), (2, 0))
+RG = range(11)
+LWB = 6
+PB, TB, YB = 3, 3, 2
+
+
+def tile_chebyshev_filter_last_term_d7_kernel(tc, L_bytes, L_scale, t1, t0, theta_bytes, theta_scale, acc, out):
+    nc = tc.nc
+    with ExitStack() as ctx:
+        keep = ctx.enter_context(tc.tile_pool(name="keep", bufs=1))
+        work = ctx.enter_context(tc.tile_pool(name="work", bufs=3))
+        psum = ctx.enter_context(tc.psum_pool(name="psum", bufs=1))
+
+        ident = keep.tile([P, P], F32, name="ident")
+        make_identity(nc, ident[:])
+
+        if True:
+            l_sc = keep.tile([P, NT * NT], F32, name="l_sc")
+            nc.scalar.dma_start(out=l_sc[:], in_=L_scale.rearrange("a b -> (a b)").partition_broadcast(P))
+            th_sc = keep.tile([P, G2, 4], F32, name="th_sc")
+            th_sc_rows = theta_scale.rearrange("(g q) o -> q g o", q=4)
+
+            l_src = L_bytes.rearrange("(c a p) j -> c p a j", a=2, p=P)
+            t1_src = t1.rearrange("(g p t) f -> g p t f", p=P, t=4)
+            t0_src = t0.rearrange("(c a p) f -> c p a f", a=2, p=P)
+            acc_src = acc.rearrange("(c a p) o -> c p a o", a=4, p=P)
+            l_by = [keep.tile([P, 2, V], U8, name="l_by%d" % c) for c in range(NP)]
+            t1_raw = [[keep.tile([P, 4, 512], BF16, name="t1_raw%d_%d" % (g, h)) for h in range(2)] for g in range(G1)]
+            t0_sb = [keep.tile([P, 2, F], BF16, name="t0_sb%d" % c) for c in range(NP)]
+            acc_sb = [keep.tile([P, 4, O], BF16, name="acc_sb%d" % c) for c in range(3)]
+            th_by = keep.tile([P, G2, 4, O], U8, name="th_by")
+
+            def load_l(c):
+                nc.sync.dma_start(out=l_by[c][:], in_=l_src[c])
+
+            def load_t1(g, h):
+                nc.sync.dma_start(out=t1_raw[g][h][:], in_=t1_src[g][:, :, 512 * h : 512 * h + 512])
+
+            def load_t0(c):
+                nc.sync.dma_start(out=t0_sb[c][:], in_=t0_src[c])
+
+            def load_acc(c):
+                nc.sync.dma_start(out=acc_sb[c][:], in_=acc_src[c])
+
+            nc.sync.dma_start(out=l_by[0][:, 0, :], in_=l_src[0][:, 0, :])
+            for f0 in (0, 256):
+                nc.sync.dma_start(out=t1_raw[0][0][:, :, f0 : f0 + 256], in_=t1_src[0][:, :, f0 : f0 + 256])
+            nc.sync.dma_start(out=l_by[0][:, 1, :], in_=l_src[0][:, 1, :])
+            load_t1(1, 0)
+            load_l(1)
+            load_t1(2, 0)
+            load_t1(0, 1)
+            load_t0(0)
+            load_t1(1, 1)
+            load_t1(2, 1)
+            load_l(2)
+            load_t0(1)
+            for q in range(4):
+                nc.sync.dma_start(out=th_sc[32 * q : 32 * q + 32], in_=th_sc_rows[q].partition_broadcast(32))
+            nc.sync.dma_start(out=th_by[:], in_=theta_bytes.rearrange("(g p t) o -> p g t o", p=P, t=4))
+            load_l(3)
+            load_t0(2)
+            load_acc(0)
+            load_l(4)
+            load_l(5)
+            load_t0(3)
+            load_acc(1)
+            load_t0(4)
+            load_t0(5)
+            load_acc(2)
+
+            t1_mx = {}
+            t1_il = {}
+
+            def t1_copy(g, h, parts=1):
+                act = (g, h) in T1A
+                il = work.tile([P, 512, 4], BF16, name="t1_il", align_bytes=64)
+                w = 512 // parts
+                for i in range(parts):
+                    dst, src = il[:, i * w : i * w + w, :], t1_raw[g][h][:, :, i * w : i * w + w].rearrange("p t f -> p f t")
+                    if act:
+                        nc.scalar.copy(out=dst, in_=src)
+                    else:
+                        nc.vector.tensor_copy(out=dst, in_=src)
+                t1_il[g, h] = il
+
+            def t1_quant(g, h):
+                q = keep.tile([P, 512], U32, name="t1_q%d_%d" % (g, h), align_bytes=64)
+                s = keep.tile([P, 512], U8, name="t1_s%d_%d" % (g, h), align_bytes=64)
+                nc.vector.quantize_mx(out=q[:].bitcast(FP8X4), scales=s[:], in_=t1_il[g, h][:].rearrange("p f t -> p (f t)"))
+                t1_mx[g, h] = (q, s)
+
+            l_w = {}
+            l_ps = {}
+            l_il = {}
+            l_mx = {}
+
+            def widen(n, b0=0, b1=NT):
+                if n not in l_w:
+                    l_w[n] = work.tile([P, V], BF16, name="l_w", bufs=LWB)
+                src = l_by[n // 2][:, n % 2, :].bitcast(FP8)
+                for b in range(b0, b1):
+                    k = NT * n + b
+                    if n in WV:
+                        g, q = divmod(b, 4)
+                        nc.vector.tensor_scalar(
+                            out=l_w[n][:].rearrange("p (g u m e) -> p g m u e", g=G1, u=2, e=2)[:, g, 32 * q : 32 * q + 32],
+                            in0=src[:, P * b : P * b + P].rearrange("p (m u e) -> p m u e", u=2, e=2),
+                            scalar1=l_sc[:, k : k + 1],
+                            scalar2=None,
+                            op0=ALU.mult,
+                        )
+                    else:
+                        nc.scalar.activation(
+                            out=l_w[n][:, P * b : P * b + P],
+                            in_=src[:, P * b : P * b + P],
+                            func=ACT.Copy,
+                            scale=l_sc[:, k : k + 1],
+                        )
+
+            def l_turn(c, g):
+                ps = psum.tile([P, 2, 2, P], F32, name="turn", bufs=TB)
+                for a in range(2):
+                    words = l_w[2 * c + a][:].bitcast(F32)
+                    for u in range(2):
+                        if 2 * c + a in WV:
+                            part = words[:, 256 * g + 128 * u : 256 * g + 128 * u + 128]
+                        else:
+                            part = words[:, 256 * g + u : 256 * (g + 1) : 2]
+                        nc.tensor.transpose(ps[:, a, u, :], part, ident[:])
+                l_ps[c, g] = ps
+
+            def l_out(c, g):
+                il = work.tile([P, 1024], BF16, name="l_il", bufs=6, align_bytes=64)
+                nc.scalar.copy(
+                    out=il[:].bitcast(F32).rearrange("p (a i u) -> p a i u", a=2, u=2),
+                    in_=l_ps[c, g][:].rearrange("p a u i -> p a i u"),
+                )
+                l_il[c, g] = il
+
+            def l_quant(c, g):
+                q = work.tile([P, 256], U32, name="l_q%d" % g, bufs=4, align_bytes=64)
+                s = work.tile([P, 256], U8, name="l_s%d" % g, bufs=4, align_bytes=64)
+                nc.vector.quantize_mx(out=q[:].bitcast(FP8X4), scales=s[:], in_=l_il[c, g][:])
+                l_mx[c, g] = (q, s)
+
+            p_ps = {}
+            z_sb = {}
+
+            def mm1(n, h):
+                ps = psum.tile([P, 512], F32, name="prod", bufs=PB)
+                cols = slice(P * (n % 2), P * (n % 2) + P)
+                for g in range(G1):
+                    lq, ls = l_mx[n // 2, g]
+                    tq, ts = t1_mx[g, h]
+                    nc.tensor.matmul_mx(
+                        out=ps[:],
+                        lhsT=lq[:, cols].bitcast(FP8X4),
+                        lhsT_scale=ls[:, cols],
+                        rhs=tq[:].bitcast(FP8X4),
+                        rhs_scale=ts[:],
+                        start=(g == 0),
+                        stop=(g == G1 - 1),
+                    )
+                p_ps[n, h] = ps
+
+            def z_step(n, h):
+                if n not in z_sb:
+                    z_sb[n] = work.tile([P, G2, 2, 256], BF16, name="z_sb", bufs=6)
+                pv = p_ps[n, h][:].rearrange("p (m u e) -> p u m e", u=2, e=2)
+                tv = t0_sb[n // 2][:, n % 2, 512 * h : 512 * h + 512].rearrange("p (m u e) -> p u m e", u=2, e=2)
+                for u in range(2):
+                    nc.vector.scalar_tensor_tensor(
+                        out=z_sb[n][:, h, u, :].rearrange("p (m e) -> p m e", e=2),
+                        in0=pv[:, u],
+                        scalar=2.0,
+                        in1=tv[:, u],
+                        op0=ALU.mult,
+                        op1=ALU.subtract,
+                    )
+
+            zt_ps = {}
+            z_il = {}
+            z_mx = {}
+
+            def z_turn(n):
+                ps = psum.tile([P, G2, 2, P], F32, name="turn", bufs=TB)
+                for g in range(G2):
+                    for u in range(2):
+                        nc.tensor.transpose(ps[:, g, u, :], z_sb[n][:, g, u, :].bitcast(F32), ident[:])
+                zt_ps[n] = ps
+
+            def z_out(n):
+                il = work.tile([P, 1024], BF16, name="z_il", align_bytes=64)
+                nc.scalar.copy(
+                    out=il[:].bitcast(F32).rearrange("p (g i u) -> p g i u", g=2, u=2),
+                    in_=zt_ps[n][:].rearrange("p g u i -> p g i u"),
+                )
+                z_il[n] = il
+
+            def z_quant(n):
+                q = work.tile([P, 256], U32, name="z_q", align_bytes=64)
+                s = work.tile([P, 256], U8, name="z_s", align_bytes=64)
+                nc.vector.quantize_mx(out=q[:].bitcast(FP8X4), scales=s[:], in_=z_il[n][:])
+                z_mx[n] = (q, s)
+
+            th_w = keep.tile([P, G2, 4, O], BF16, name="th_w")
+            th_il = keep.tile([P, G2, O, 4], BF16, name="th_il", align_bytes=64)
+            th_q = keep.tile([P, G2, O], U32, name="th_q", align_bytes=64)
+            th_s = keep.tile([P, G2, O], U8, name="th_s", align_bytes=64)
+
+            def th_widen(g):
+                nc.scalar.copy(
+                    out=th_w[:, g].rearrange("p t o -> p (t o)"), in_=th_by[:, g].rearrange("p t o -> p (t o)").bitcast(FP8)
+                )
+
+            def th_scale(g):
+                for b in range(4):
+                    nc.vector.tensor_scalar(
+                        out=th_il[:, g, P * b : P * b + P, :],
+                        in0=th_w[:, g, :, P * b : P * b + P].rearrange("p t o -> p o t"),
+                        scalar1=th_sc[:, g, b : b + 1],
+                        scalar2=None,
+                        op0=ALU.mult,
+                    )
+
+            def th_quant(g):
+                nc.vector.quantize_mx(
+                    out=th_q[:, g].bitcast(FP8X4), scales=th_s[:, g], in_=th_il[:, g].rearrange("p o t -> p (o t)")
+                )
+
+            y_ps = {}
+            sums = {}
+
+            def mm2(n):
+                ps = psum.tile([P, O], F32, name="y", bufs=YB)
+                zq, zs = z_mx[n]
+                for g in range(G2):
+                    cols = slice(P * g, P * g + P)
+                    nc.tensor.matmul_mx(
+                        out=ps[:],
+                        lhsT=zq[:, cols].bitcast(FP8X4),
+                        lhsT_scale=zs[:, cols],
+                        rhs=th_q[:, g].bitcast(FP8X4),
+                        rhs_scale=th_s[:, g],
+                        start=(g == 0),
+                        stop=(g == G2 - 1),
+                    )
+                y_ps[n] = ps
+
+            def add_acc(n):
+                t = work.tile([P, O], F32, name="sums")
+                nc.vector.tensor_tensor(out=t[:], in0=y_ps[n][:], in1=acc_sb[n // 4][:, n % 4, :], op=ALU.add)
+                sums[n] = t
+
+            def relu_store(n):
+                r = work.tile([P, O], F32, name="res")
+                if n in RG:
+                    nc.gpsimd.tensor_scalar(out=r[:], in0=sums[n][:], scalar1=0.0, scalar2=0.0, op0=ALU.max, op1=ALU.add)
+                else:
+                    nc.scalar.activation(out=r[:], in_=sums[n][:], func=ACT.Relu)
+                nc.sync.dma_start(out=out[P * n : P * n + P, :], in_=r[:])
+
+            all_g = range(G1)
+            widen(0)
+            widen(1)
+            t1_copy(0, 0, parts=2)
+            t1_copy(1, 0)
+            t1_quant(0, 0)
+            for g in all_g:
+                l_turn(0, g)
+            widen(2, 0, 4)
+            for g in all_g:
+                l_out(0, g)
+            t1_copy(2, 0)
+            t1_quant(1, 0)
+            l_quant(0, 0)
+            l_quant(0, 1)
+            t1_quant(2, 0)
+            l_quant(0, 2)
+            mm1(0, 0)
+            mm1(1, 0)
+            widen(2, 4, 12)
+            widen(3)
+            for g in all_g:
+                l_turn(1, g)
+            t1_copy(0, 1)
+            z_step(0, 0)
+            t1_quant(0, 1)
+            z_step(1, 0)
+            t1_copy(1, 1)
+            for g in all_g:
+                l_out(1, g)
+            for g in all_g:
+                l_quant(1, g)
+            t1_quant(1, 1)
+            mm1(2, 0)
+            mm1(3, 0)
+            t1_copy(2, 1)
+            z_step(2, 0)
+            t1_quant(2, 1)
+            z_step(3, 0)
+            widen(4)
+            th_widen(0)
+            th_widen(1)
+
+            turned = []
+            for n in range(NT + 4):
+                if n < NT:
+                    if n >= HEAD:
+                        mm1(n, 0)
+                    mm1(n, 1)
+                outs = turned
+                turned = []
+                for c, g in outs:
+                    l_out(c, g)
+                if 2 <= n < NT + 2:
+                    z_out(n - 2)
+                if n + 5 < NT:
+                    widen(n + 5, 0, 6)
+                if n < NT:
+                    if n >= HEAD:
+                        z_step(n, 0)
+                for c, g in outs:
+                    l_quant(c, g)
+                if n < NT:
+                    z_step(n, 1)
+                if 2 <= n < NT + 2:
+                    z_quant(n - 2)
+                if n in (0, 1):
+                    th_scale(n)
+                    th_quant(n)
+                if 3 <= n < NT + 3:
+                    mm2(n - 3)
+                    add_acc(n - 3)
+                if n >= 4:
+                    relu_store(n - 4)
+                if n + 5 < NT:
+                    widen(n + 5, 6, 12)
+                if 1 <= n <= NT:
+                    z_turn(n - 1)
+                c = (n + 3) // 2
+                if 2 <= c < NP:
+                    for g in (0, 1) if n % 2 else (2,):
+                        l_turn(c, g)
+                        turned.append((c, g))

@@ -21,11 +21,12 @@ NP = NT // 2
 G1 = V // 512
 G2 = F // 512
 HEAD = 4
-WV = (0, 3, 4, 5, 7, 9, 10)
-T1A = ((1, 1), (2, 0))
-RG = range(11)
+WV = ()
+T1A = ()
+RG = ()
+RD = ()
 LWB = 6
-PB, TB, YB = 3, 3, 2
+PB, TB, YB = 4, 3, 1
 
 
 def tile_chebyshev_filter_last_term_d7_kernel(tc, L_bytes, L_scale, t1, t0, theta_bytes, theta_scale, acc, out):
@@ -207,26 +208,30 @@ def tile_chebyshev_filter_last_term_d7_kernel(tc, L_bytes, L_scale, t1, t0, thet
             z_il = {}
             z_mx = {}
 
-            def z_turn(n):
-                ps = psum.tile([P, G2, 2, P], F32, name="turn", bufs=TB)
-                for g in range(G2):
+            def z_turn(n, gs=(0, 1)):
+                if n not in zt_ps:
+                    zt_ps[n] = psum.tile([P, G2, 2, P], F32, name="turn", bufs=TB)
+                for g in gs:
                     for u in range(2):
-                        nc.tensor.transpose(ps[:, g, u, :], z_sb[n][:, g, u, :].bitcast(F32), ident[:])
-                zt_ps[n] = ps
+                        nc.tensor.transpose(zt_ps[n][:, g, u, :], z_sb[n][:, g, u, :].bitcast(F32), ident[:])
 
-            def z_out(n):
-                il = work.tile([P, 1024], BF16, name="z_il", align_bytes=64)
+            def z_out(n, gs=(0, 1)):
+                if n not in z_il:
+                    z_il[n] = work.tile([P, 1024], BF16, name="z_il", align_bytes=64)
+                a, b = gs[0], gs[-1] + 1
                 nc.scalar.copy(
-                    out=il[:].bitcast(F32).rearrange("p (g i u) -> p g i u", g=2, u=2),
-                    in_=zt_ps[n][:].rearrange("p g u i -> p g i u"),
+                    out=z_il[n][:].bitcast(F32).rearrange("p (g i u) -> p g i u", g=2, u=2)[:, a:b],
+                    in_=zt_ps[n][:].rearrange("p g u i -> p g i u")[:, a:b],
                 )
-                z_il[n] = il
 
-            def z_quant(n):
-                q = work.tile([P, 256], U32, name="z_q", align_bytes=64)
-                s = work.tile([P, 256], U8, name="z_s", align_bytes=64)
-                nc.vector.quantize_mx(out=q[:].bitcast(FP8X4), scales=s[:], in_=z_il[n][:])
-                z_mx[n] = (q, s)
+            def z_quant(n, gs=(0, 1)):
+                if n not in z_mx:
+                    q = work.tile([P, 256], U32, name="z_q", align_bytes=64)
+                    s = work.tile([P, 256], U8, name="z_s", align_bytes=64)
+                    z_mx[n] = (q, s)
+                q, s = z_mx[n]
+                a, b = P * gs[0], P * (gs[-1] + 1)
+                nc.vector.quantize_mx(out=q[:, a:b].bitcast(FP8X4), scales=s[:, a:b], in_=z_il[n][:, 4 * a : 4 * b])
 
             th_w = keep.tile([P, G2, 4, O], BF16, name="th_w")
             th_il = keep.tile([P, G2, O, 4], BF16, name="th_il", align_bytes=64)
@@ -256,13 +261,14 @@ def tile_chebyshev_filter_last_term_d7_kernel(tc, L_bytes, L_scale, t1, t0, thet
             y_ps = {}
             sums = {}
 
-            def mm2(n):
-                ps = psum.tile([P, O], F32, name="y", bufs=YB)
+            def mm2(n, gs=(0, 1)):
+                if n not in y_ps:
+                    y_ps[n] = psum.tile([P, O], F32, name="y", bufs=YB)
                 zq, zs = z_mx[n]
-                for g in range(G2):
+                for g in gs:
                     cols = slice(P * g, P * g + P)
                     nc.tensor.matmul_mx(
-                        out=ps[:],
+                        out=y_ps[n][:],
                         lhsT=zq[:, cols].bitcast(FP8X4),
                         lhsT_scale=zs[:, cols],
                         rhs=th_q[:, g].bitcast(FP8X4),
@@ -270,20 +276,25 @@ def tile_chebyshev_filter_last_term_d7_kernel(tc, L_bytes, L_scale, t1, t0, thet
                         start=(g == 0),
                         stop=(g == G2 - 1),
                     )
-                y_ps[n] = ps
 
-            def add_acc(n):
+            def add_acc(n, parts=1):
                 t = work.tile([P, O], F32, name="sums")
-                nc.vector.tensor_tensor(out=t[:], in0=y_ps[n][:], in1=acc_sb[n // 4][:, n % 4, :], op=ALU.add)
+                for i in range(parts):
+                    w = slice(i * O // parts, (i + 1) * O // parts)
+                    nc.vector.tensor_tensor(out=t[:, w], in0=y_ps[n][:, w], in1=acc_sb[n // 4][:, n % 4, w], op=ALU.add)
                 sums[n] = t
 
-            def relu_store(n):
+            def relu_store(n, parts=1):
                 r = work.tile([P, O], F32, name="res")
-                if n in RG:
-                    nc.gpsimd.tensor_scalar(out=r[:], in0=sums[n][:], scalar1=0.0, scalar2=0.0, op0=ALU.max, op1=ALU.add)
-                else:
-                    nc.scalar.activation(out=r[:], in_=sums[n][:], func=ACT.Relu)
-                nc.sync.dma_start(out=out[P * n : P * n + P, :], in_=r[:])
+                for i in range(parts):
+                    w = slice(i * O // parts, (i + 1) * O // parts)
+                    if n in RG:
+                        nc.gpsimd.tensor_scalar(out=r[:, w], in0=sums[n][:, w], scalar1=0.0, scalar2=0.0, op0=ALU.max, op1=ALU.add)
+                    elif n in RD:
+                        nc.vector.tensor_scalar(out=r[:, w], in0=sums[n][:, w], scalar1=0.0, scalar2=None, op0=ALU.max)
+                    else:
+                        nc.scalar.activation(out=r[:, w], in_=sums[n][:, w], func=ACT.Relu)
+                    nc.sync.dma_start(out=out[P * n : P * n + P, w], in_=r[:, w])
 
             all_g = range(G1)
             widen(0)
@@ -329,6 +340,7 @@ def tile_chebyshev_filter_last_term_d7_kernel(tc, L_bytes, L_scale, t1, t0, thet
             th_widen(1)
 
             turned = []
+            last = NT - 1
             for n in range(NT + 4):
                 if n < NT:
                     if n >= HEAD:
@@ -338,8 +350,11 @@ def tile_chebyshev_filter_last_term_d7_kernel(tc, L_bytes, L_scale, t1, t0, thet
                 turned = []
                 for c, g in outs:
                     l_out(c, g)
-                if 2 <= n < NT + 2:
+                if 2 <= n < NT + 1:
                     z_out(n - 2)
+                if n == NT + 1:
+                    for g in range(G2):
+                        z_out(last, (g,))
                 if n + 5 < NT:
                     widen(n + 5, 0, 6)
                 if n < NT:
@@ -349,20 +364,26 @@ def tile_chebyshev_filter_last_term_d7_kernel(tc, L_bytes, L_scale, t1, t0, thet
                     l_quant(c, g)
                 if n < NT:
                     z_step(n, 1)
-                if 2 <= n < NT + 2:
+                if 2 <= n < NT + 1:
                     z_quant(n - 2)
+                if n == NT + 1:
+                    for g in range(G2):
+                        z_quant(last, (g,))
                 if n in (0, 1):
                     th_scale(n)
                     th_quant(n)
                 if 3 <= n < NT + 3:
                     mm2(n - 3)
-                    add_acc(n - 3)
+                    add_acc(n - 3, 2 if n - 3 == last else 1)
                 if n >= 4:
-                    relu_store(n - 4)
+                    relu_store(n - 4, 2 if n - 4 == last else 1)
                 if n + 5 < NT:
                     widen(n + 5, 6, 12)
-                if 1 <= n <= NT:
+                if 1 <= n < NT:
                     z_turn(n - 1)
+                if n == NT:
+                    for g in range(G2):
+                        z_turn(last, (g,))
                 c = (n + 3) // 2
                 if 2 <= c < NP:
                     for g in (0, 1) if n % 2 else (2,):

from contextlib import ExitStack

import concourse.mybir as mybir
from concourse.masks import make_identity

V, F, O = 1536, 1024, 512
FLOPS = 2 * V * V * F + 2 * V * F * O

F32 = mybir.dt.float32
BF16 = mybir.dt.bfloat16
U32 = mybir.dt.uint32
U8 = mybir.dt.uint8
FP8 = mybir.dt.float8_e4m3fn
FP8X4 = mybir.dt.float8_e4m3fn_x4
ACT = mybir.ActivationFunctionType
ALU = mybir.AluOpType

P = 128
NT = V // P
NP = NT // 2
G1 = V // 512
G2 = F // 512
HEAD = 4
WV = ()
T1A = ()
RG = ()
RD = ()
LWB = 6
PB, TB, YB = 4, 3, 1


def tile_chebyshev_filter_last_term_d7_kernel(tc, L_bytes, L_scale, t1, t0, theta_bytes, theta_scale, acc, out):
    nc = tc.nc
    with ExitStack() as ctx:
        keep = ctx.enter_context(tc.tile_pool(name="keep", bufs=1))
        work = ctx.enter_context(tc.tile_pool(name="work", bufs=3))
        psum = ctx.enter_context(tc.psum_pool(name="psum", bufs=1))

        ident = keep.tile([P, P], F32, name="ident")
        make_identity(nc, ident[:])

        if True:
            l_sc = keep.tile([P, NT * NT], F32, name="l_sc")
            nc.scalar.dma_start(out=l_sc[:], in_=L_scale.rearrange("a b -> (a b)").partition_broadcast(P))
            th_sc = keep.tile([P, G2, 4], F32, name="th_sc")
            th_sc_rows = theta_scale.rearrange("(g q) o -> q g o", q=4)

            l_src = L_bytes.rearrange("(c a p) j -> c p a j", a=2, p=P)
            t1_src = t1.rearrange("(g p t) f -> g p t f", p=P, t=4)
            t0_src = t0.rearrange("(c a p) f -> c p a f", a=2, p=P)
            acc_src = acc.rearrange("(c a p) o -> c p a o", a=4, p=P)
            l_by = [keep.tile([P, 2, V], U8, name="l_by%d" % c) for c in range(NP)]
            t1_raw = [[keep.tile([P, 4, 512], BF16, name="t1_raw%d_%d" % (g, h)) for h in range(2)] for g in range(G1)]
            t0_sb = [keep.tile([P, 2, F], BF16, name="t0_sb%d" % c) for c in range(NP)]
            acc_sb = [keep.tile([P, 4, O], BF16, name="acc_sb%d" % c) for c in range(3)]
            th_by = keep.tile([P, G2, 4, O], U8, name="th_by")

            def load_l(c):
                nc.sync.dma_start(out=l_by[c][:], in_=l_src[c])

            def load_t1(g, h):
                nc.sync.dma_start(out=t1_raw[g][h][:], in_=t1_src[g][:, :, 512 * h : 512 * h + 512])

            def load_t0(c):
                nc.sync.dma_start(out=t0_sb[c][:], in_=t0_src[c])

            def load_acc(c):
                nc.sync.dma_start(out=acc_sb[c][:], in_=acc_src[c])

            nc.sync.dma_start(out=l_by[0][:, 0, :], in_=l_src[0][:, 0, :])
            for f0 in (0, 256):
                nc.sync.dma_start(out=t1_raw[0][0][:, :, f0 : f0 + 256], in_=t1_src[0][:, :, f0 : f0 + 256])
            nc.sync.dma_start(out=l_by[0][:, 1, :], in_=l_src[0][:, 1, :])
            load_t1(1, 0)
            load_l(1)
            load_t1(2, 0)
            load_t1(0, 1)
            load_t0(0)
            load_t1(1, 1)
            load_t1(2, 1)
            load_l(2)
            load_t0(1)
            for q in range(4):
                nc.sync.dma_start(out=th_sc[32 * q : 32 * q + 32], in_=th_sc_rows[q].partition_broadcast(32))
            nc.sync.dma_start(out=th_by[:], in_=theta_bytes.rearrange("(g p t) o -> p g t o", p=P, t=4))
            load_l(3)
            load_t0(2)
            load_acc(0)
            load_l(4)
            load_l(5)
            load_t0(3)
            load_acc(1)
            load_t0(4)
            load_t0(5)
            load_acc(2)

            t1_mx = {}
            t1_il = {}

            def t1_copy(g, h, parts=1):
                act = (g, h) in T1A
                il = work.tile([P, 512, 4], BF16, name="t1_il", align_bytes=64)
                w = 512 // parts
                for i in range(parts):
                    dst, src = il[:, i * w : i * w + w, :], t1_raw[g][h][:, :, i * w : i * w + w].rearrange("p t f -> p f t")
                    if act:
                        nc.scalar.copy(out=dst, in_=src)
                    else:
                        nc.vector.tensor_copy(out=dst, in_=src)
                t1_il[g, h] = il

            def t1_quant(g, h):
                q = keep.tile([P, 512], U32, name="t1_q%d_%d" % (g, h), align_bytes=64)
                s = keep.tile([P, 512], U8, name="t1_s%d_%d" % (g, h), align_bytes=64)
                nc.vector.quantize_mx(out=q[:].bitcast(FP8X4), scales=s[:], in_=t1_il[g, h][:].rearrange("p f t -> p (f t)"))
                t1_mx[g, h] = (q, s)

            l_w = {}
            l_ps = {}
            l_il = {}
            l_mx = {}

            def widen(n, b0=0, b1=NT):
                if n not in l_w:
                    l_w[n] = work.tile([P, V], BF16, name="l_w", bufs=LWB)
                src = l_by[n // 2][:, n % 2, :].bitcast(FP8)
                for b in range(b0, b1):
                    k = NT * n + b
                    if n in WV:
                        g, q = divmod(b, 4)
                        nc.vector.tensor_scalar(
                            out=l_w[n][:].rearrange("p (g u m e) -> p g m u e", g=G1, u=2, e=2)[:, g, 32 * q : 32 * q + 32],
                            in0=src[:, P * b : P * b + P].rearrange("p (m u e) -> p m u e", u=2, e=2),
                            scalar1=l_sc[:, k : k + 1],
                            scalar2=None,
                            op0=ALU.mult,
                        )
                    else:
                        nc.scalar.activation(
                            out=l_w[n][:, P * b : P * b + P],
                            in_=src[:, P * b : P * b + P],
                            func=ACT.Copy,
                            scale=l_sc[:, k : k + 1],
                        )

            def l_turn(c, g):
                ps = psum.tile([P, 2, 2, P], F32, name="turn", bufs=TB)
                for a in range(2):
                    words = l_w[2 * c + a][:].bitcast(F32)
                    for u in range(2):
                        if 2 * c + a in WV:
                            part = words[:, 256 * g + 128 * u : 256 * g + 128 * u + 128]
                        else:
                            part = words[:, 256 * g + u : 256 * (g + 1) : 2]
                        nc.tensor.transpose(ps[:, a, u, :], part, ident[:])
                l_ps[c, g] = ps

            def l_out(c, g):
                il = work.tile([P, 1024], BF16, name="l_il", bufs=6, align_bytes=64)
                nc.scalar.copy(
                    out=il[:].bitcast(F32).rearrange("p (a i u) -> p a i u", a=2, u=2),
                    in_=l_ps[c, g][:].rearrange("p a u i -> p a i u"),
                )
                l_il[c, g] = il

            def l_quant(c, g):
                q = work.tile([P, 256], U32, name="l_q%d" % g, bufs=4, align_bytes=64)
                s = work.tile([P, 256], U8, name="l_s%d" % g, bufs=4, align_bytes=64)
                nc.vector.quantize_mx(out=q[:].bitcast(FP8X4), scales=s[:], in_=l_il[c, g][:])
                l_mx[c, g] = (q, s)

            p_ps = {}
            z_sb = {}

            def mm1(n, h):
                ps = psum.tile([P, 512], F32, name="prod", bufs=PB)
                cols = slice(P * (n % 2), P * (n % 2) + P)
                for g in range(G1):
                    lq, ls = l_mx[n // 2, g]
                    tq, ts = t1_mx[g, h]
                    nc.tensor.matmul_mx(
                        out=ps[:],
                        lhsT=lq[:, cols].bitcast(FP8X4),
                        lhsT_scale=ls[:, cols],
                        rhs=tq[:].bitcast(FP8X4),
                        rhs_scale=ts[:],
                        start=(g == 0),
                        stop=(g == G1 - 1),
                    )
                p_ps[n, h] = ps

            def z_step(n, h):
                if n not in z_sb:
                    z_sb[n] = work.tile([P, G2, 2, 256], BF16, name="z_sb", bufs=6)
                pv = p_ps[n, h][:].rearrange("p (m u e) -> p u m e", u=2, e=2)
                tv = t0_sb[n // 2][:, n % 2, 512 * h : 512 * h + 512].rearrange("p (m u e) -> p u m e", u=2, e=2)
                for u in range(2):
                    nc.vector.scalar_tensor_tensor(
                        out=z_sb[n][:, h, u, :].rearrange("p (m e) -> p m e", e=2),
                        in0=pv[:, u],
                        scalar=2.0,
                        in1=tv[:, u],
                        op0=ALU.mult,
                        op1=ALU.subtract,
                    )

            zt_ps = {}
            z_il = {}
            z_mx = {}

            def z_turn(n, gs=(0, 1)):
                if n not in zt_ps:
                    zt_ps[n] = psum.tile([P, G2, 2, P], F32, name="turn", bufs=TB)
                for g in gs:
                    for u in range(2):
                        nc.tensor.transpose(zt_ps[n][:, g, u, :], z_sb[n][:, g, u, :].bitcast(F32), ident[:])

            def z_out(n, gs=(0, 1)):
                if n not in z_il:
                    z_il[n] = work.tile([P, 1024], BF16, name="z_il", align_bytes=64)
                a, b = gs[0], gs[-1] + 1
                nc.scalar.copy(
                    out=z_il[n][:].bitcast(F32).rearrange("p (g i u) -> p g i u", g=2, u=2)[:, a:b],
                    in_=zt_ps[n][:].rearrange("p g u i -> p g i u")[:, a:b],
                )

            def z_quant(n, gs=(0, 1)):
                if n not in z_mx:
                    q = work.tile([P, 256], U32, name="z_q", align_bytes=64)
                    s = work.tile([P, 256], U8, name="z_s", align_bytes=64)
                    z_mx[n] = (q, s)
                q, s = z_mx[n]
                a, b = P * gs[0], P * (gs[-1] + 1)
                nc.vector.quantize_mx(out=q[:, a:b].bitcast(FP8X4), scales=s[:, a:b], in_=z_il[n][:, 4 * a : 4 * b])

            th_w = keep.tile([P, G2, 4, O], BF16, name="th_w")
            th_il = keep.tile([P, G2, O, 4], BF16, name="th_il", align_bytes=64)
            th_q = keep.tile([P, G2, O], U32, name="th_q", align_bytes=64)
            th_s = keep.tile([P, G2, O], U8, name="th_s", align_bytes=64)

            def th_widen(g):
                nc.scalar.copy(
                    out=th_w[:, g].rearrange("p t o -> p (t o)"), in_=th_by[:, g].rearrange("p t o -> p (t o)").bitcast(FP8)
                )

            def th_scale(g):
                for b in range(4):
                    nc.vector.tensor_scalar(
                        out=th_il[:, g, P * b : P * b + P, :],
                        in0=th_w[:, g, :, P * b : P * b + P].rearrange("p t o -> p o t"),
                        scalar1=th_sc[:, g, b : b + 1],
                        scalar2=None,
                        op0=ALU.mult,
                    )

            def th_quant(g):
                nc.vector.quantize_mx(
                    out=th_q[:, g].bitcast(FP8X4), scales=th_s[:, g], in_=th_il[:, g].rearrange("p o t -> p (o t)")
                )

            y_ps = {}
            sums = {}

            def mm2(n, gs=(0, 1)):
                if n not in y_ps:
                    y_ps[n] = psum.tile([P, O], F32, name="y", bufs=YB)
                zq, zs = z_mx[n]
                for g in gs:
                    cols = slice(P * g, P * g + P)
                    nc.tensor.matmul_mx(
                        out=y_ps[n][:],
                        lhsT=zq[:, cols].bitcast(FP8X4),
                        lhsT_scale=zs[:, cols],
                        rhs=th_q[:, g].bitcast(FP8X4),
                        rhs_scale=th_s[:, g],
                        start=(g == 0),
                        stop=(g == G2 - 1),
                    )

            def add_acc(n, parts=1):
                t = work.tile([P, O], F32, name="sums")
                for i in range(parts):
                    w = slice(i * O // parts, (i + 1) * O // parts)
                    nc.vector.tensor_tensor(out=t[:, w], in0=y_ps[n][:, w], in1=acc_sb[n // 4][:, n % 4, w], op=ALU.add)
                sums[n] = t

            def relu_store(n, parts=1):
                r = work.tile([P, O], F32, name="res")
                for i in range(parts):
                    w = slice(i * O // parts, (i + 1) * O // parts)
                    if n in RG:
                        nc.gpsimd.tensor_scalar(out=r[:, w], in0=sums[n][:, w], scalar1=0.0, scalar2=0.0, op0=ALU.max, op1=ALU.add)
                    elif n in RD:
                        nc.vector.tensor_scalar(out=r[:, w], in0=sums[n][:, w], scalar1=0.0, scalar2=None, op0=ALU.max)
                    else:
                        nc.scalar.activation(out=r[:, w], in_=sums[n][:, w], func=ACT.Relu)
                    nc.sync.dma_start(out=out[P * n : P * n + P, w], in_=r[:, w])

            all_g = range(G1)
            widen(0)
            widen(1)
            t1_copy(0, 0, parts=2)
            t1_copy(1, 0)
            t1_quant(0, 0)
            for g in all_g:
                l_turn(0, g)
            widen(2, 0, 4)
            for g in all_g:
                l_out(0, g)
            t1_copy(2, 0)
            t1_quant(1, 0)
            l_quant(0, 0)
            l_quant(0, 1)
            t1_quant(2, 0)
            l_quant(0, 2)
            mm1(0, 0)
            mm1(1, 0)
            widen(2, 4, 12)
            widen(3)
            for g in all_g:
                l_turn(1, g)
            t1_copy(0, 1)
            z_step(0, 0)
            t1_quant(0, 1)
            z_step(1, 0)
            t1_copy(1, 1)
            for g in all_g:
                l_out(1, g)
            for g in all_g:
                l_quant(1, g)
            t1_quant(1, 1)
            mm1(2, 0)
            mm1(3, 0)
            t1_copy(2, 1)
            z_step(2, 0)
            t1_quant(2, 1)
            z_step(3, 0)
            widen(4)
            th_widen(0)
            th_widen(1)

            turned = []
            last = NT - 1
            for n in range(NT + 4):
                if n < NT:
                    if n >= HEAD:
                        mm1(n, 0)
                    mm1(n, 1)
                outs = turned
                turned = []
                for c, g in outs:
                    l_out(c, g)
                if 2 <= n < NT + 1:
                    z_out(n - 2)
                if n == NT + 1:
                    for g in range(G2):
                        z_out(last, (g,))
                if n + 5 < NT:
                    widen(n + 5, 0, 6)
                if n < NT:
                    if n >= HEAD:
                        z_step(n, 0)
                for c, g in outs:
                    l_quant(c, g)
                if n < NT:
                    z_step(n, 1)
                if 2 <= n < NT + 1:
                    z_quant(n - 2)
                if n == NT + 1:
                    for g in range(G2):
                        z_quant(last, (g,))
                if n in (0, 1):
                    th_scale(n)
                    th_quant(n)
                if 3 <= n < NT + 3:
                    mm2(n - 3)
                    add_acc(n - 3, 2 if n - 3 == last else 1)
                if n >= 4:
                    relu_store(n - 4, 2 if n - 4 == last else 1)
                if n + 5 < NT:
                    widen(n + 5, 6, 12)
                if 1 <= n < NT:
                    z_turn(n - 1)
                if n == NT:
                    for g in range(G2):
                        z_turn(last, (g,))
                c = (n + 3) // 2
                if 2 <= c < NP:
                    for g in (0, 1) if n % 2 else (2,):
                        l_turn(c, g)
                        turned.append((c, g))
